import numpy as np
import ml_dtypes


def mxq(x, axis, fmt="e4m3"):
    dtype, down = {"e4m3": (ml_dtypes.float8_e4m3fn, 7), "e5m2": (ml_dtypes.float8_e5m2, 14)}[fmt]
    v = np.moveaxis(np.asarray(x, np.float32).astype(ml_dtypes.bfloat16).astype(np.float64), axis, -1)
    blocks = v.reshape(v.shape[:-1] + (-1, 32))
    amax = np.abs(blocks).max(-1, keepdims=True)
    byte = np.maximum(np.where(amax > 0, np.frexp(amax)[1] - 1 + 127, 0) - down, 1)
    scale = np.exp2(byte - 127.0)
    codes = (blocks / scale).astype(np.float32).astype(dtype).astype(np.float64)
    return np.moveaxis((codes * scale).reshape(v.shape), -1, axis)


WIDE = False


def mx_kscale(k):
    if not WIDE:
        return np.ones(k)
    levels = np.array([10, -10, 5, -5, 0])
    if k % 512:
        return np.exp2(np.random.permutation(np.resize(levels, k // 32))).repeat(32)
    a = np.empty((k // 512, 16))
    for p in range(k // 512):
        a[p, :8] = np.random.permutation(np.resize(levels, 8))
        for g in range(8):
            far = levels[np.abs(levels - a[p, g]) >= 10]
            a[p, g + 8] = far[np.random.randint(len(far))]
    return np.exp2(a.ravel()).repeat(32)


def f64(x):
    return np.asarray(x).astype(np.float64)


E2M1 = np.array([0.0, 0.5, 1.0, 1.5, 2.0, 3.0, 4.0, 6.0, -0.0, -0.5, -1.0, -1.5, -2.0, -3.0, -4.0, -6.0])


def pack_weight(w, fmt):
    k, n = w.shape
    w = f64(np.asarray(w, np.float32).astype(ml_dtypes.bfloat16)).reshape(k // 32, 32, n)
    amax = np.abs(w).max(1)
    if fmt == "e4m3":
        byte = np.frexp(amax)[1] - 1 + 127 - 7
    else:
        mant, ex = np.frexp(amax / 6.0)
        byte = np.where(mant > 0.5, ex, ex - 1) + 127
    byte = np.clip(np.where(amax > 0, byte, 1), 1, 254)
    scaled = (w * np.exp2(127.0 - byte)[:, None, :]).reshape(k, n).astype(np.float32)
    by_word = np.ascontiguousarray(scaled.reshape(k // 512, 128, 4, n).transpose(0, 1, 3, 2))
    if fmt == "e4m3":
        words = by_word.astype(ml_dtypes.float8_e4m3fn).view(np.uint8)
    else:
        c = by_word.astype(ml_dtypes.float4_e2m1fn).view(np.uint8) & 0xF
        words = (c[..., 0::2] | (c[..., 1::2] << 4)).reshape(k // 512, 128, 2 * n)
    return np.ascontiguousarray(words), np.ascontiguousarray(byte.astype(np.uint8).reshape(k // 512, 16, n))


def unpack_weight(words, scales, fmt):
    g, _, n = scales.shape
    words = np.ascontiguousarray(words).reshape(g, 128, n, -1)
    if fmt == "e4m3":
        vals = words.view(ml_dtypes.float8_e4m3fn).astype(np.float64)
    else:
        nib = np.empty((g, 128, n, 4), np.uint8)
        nib[..., 0::2] = words & 0xF
        nib[..., 1::2] = words >> 4
        vals = E2M1[nib]
    vals = vals * np.repeat(np.exp2(scales.astype(np.float64) - 127.0), 8, axis=1)[..., None]
    return vals.transpose(0, 1, 3, 2).reshape(g * 512, n)


K, M, T = 512, 1536, 1024


def setup_inputs():
    n = np.random.standard_normal
    s = mx_kscale(K)[:, None]
    x = n((K, T)) * s
    x4 = pack_weight(x, "e2m1")
    rest = x - unpack_weight(*x4, "e2m1")
    p_w4 = pack_weight(n((K, M)) / np.sqrt(K) / s, "e2m1")
    return {
        "x4_words": x4[0],
        "x4_scales": x4[1],
        "xr": (rest).astype(np.float32),
        "w4_words": p_w4[0],
        "w4_scales": p_w4[1],
        "b": (0.3 * n(1536)).astype(np.float32),
    }


def reference(x4_words, x4_scales, xr, w4_words, w4_scales, b):
    x4_ = unpack_weight(x4_words, x4_scales, "e2m1")
    xr_ = mxq(f64(xr), 0, "e4m3")
    w4_ = unpack_weight(w4_words, w4_scales, "e2m1")
    y = w4_.T @ x4_ + w4_.T @ xr_
    return y + f64(b)[:, None]

@@ -1,0 +1,186 @@
+from contextlib import ExitStack
+
+import concourse.mybir as mybir
+
+F32 = mybir.dt.float32
+BF16 = mybir.dt.bfloat16
+U32 = mybir.dt.uint32
+I32 = mybir.dt.int32
+U8 = mybir.dt.uint8
+FP8X4 = mybir.dt.float8_e4m3fn_x4
+FP4X4 = mybir.dt.float4_e2m1fn_x4
+
+P = 128
+K = 512
+M = 1536
+T = 1024
+HALF = 512
+TILES = M // P
+FLOPS = 2 * 2 * K * M * T
+
+SOLO = 4
+LEAD = 4
+V_COLS = 320
+QCOLS = 256
+
+
+def tile_mix_xres_fm_bias_kernel(tc, x4_words, x4_scales, xr, w4_words, w4_scales, b, out):
+    nc = tc.nc
+    with ExitStack() as ctx:
+        keep = ctx.enter_context(tc.tile_pool(name="keep", bufs=1))
+        outs = ctx.enter_context(tc.tile_pool(name="outs", bufs=TILES))
+        psum = ctx.enter_context(tc.psum_pool(name="psum", bufs=8))
+        ctx.enter_context(tc.manual_schedule())
+
+        warm = keep.tile([P, 1], F32, name="warm")
+        x4_plane = keep.tile([P, T], U8, name="x4_plane", align_bytes=256)
+        w4_plane = keep.tile([P, M], U8, name="w4_plane", align_bytes=256)
+        b_rows = []
+        b_cols = []
+        for i in range(2):
+            rows = keep.tile([P, 32], F32, name="b_rows%d" % i, align_bytes=256)
+            cols = keep.tile([P, 32], F32, name="b_cols%d" % i, align_bytes=256)
+            b_rows.append(rows)
+            b_cols.append(cols)
+        x4_t = keep.tile([P, 2 * T], U8, name="x4_t", align_bytes=256)
+        w4_t = keep.tile([P, 2 * M], U8, name="w4_t", align_bytes=256)
+        codes = keep.tile([P, T], U32, name="codes", align_bytes=256)
+        scales = keep.tile([P, T], U8, name="scales", align_bytes=256)
+        raw = []
+        grouped = []
+        for h in range(2):
+            r = keep.tile([P, 4, HALF], F32, name="raw%d" % h, align_bytes=256)
+            g = keep.tile([P, HALF, 4], BF16, name="grouped%d" % h, align_bytes=256)
+            raw.append(r)
+            grouped.append(g)
+
+        nc.vector.memset(warm[:], 0.0)
+        nc.vector.memset(x4_plane[:].bitcast(I32), 0)
+        nc.vector.memset(w4_plane[:].bitcast(I32), 0)
+        nc.vector.memset(b_rows[0][:], 0.0)
+        nc.vector.memset(b_rows[1][:], 0.0)
+
+        def load_scales(queue, plane, rows):
+            for q in range(4):
+                queue.dma_start(
+                    out=plane[32 * q : 32 * q + 4, :].bitcast(I32),
+                    in_=rows[0, 4 * q : 4 * q + 4, :].bitcast(I32),
+                )
+
+        def load_xr(h):
+            nc.sync.dma_start(
+                out=raw[h][:],
+                in_=xr[:, HALF * h : HALF * (h + 1)].rearrange("(p j) t -> p j t", j=4),
+            )
+
+        b_parts = b.rearrange("(k a i) -> a k i", a=4, i=32)
+        split = 2 * P * SOLO
+        nc.sync.dma_start(out=w4_t[:, 0:split], in_=w4_words[0, :, 0:split])
+        nc.sync.dma_start(out=x4_t[:], in_=x4_words[0])
+        load_xr(0)
+        load_scales(nc.scalar, x4_plane, x4_scales)
+        load_scales(nc.gpsimd, w4_plane, w4_scales)
+        nc.scalar.dma_start(out=b_rows[0][0:P:4, :], in_=b_parts[:, 0:8, :])
+        nc.gpsimd.dma_start(out=b_rows[1][0:P:8, :], in_=b_parts[:, 8:12, :])
+        load_xr(1)
+        nc.sync.dma_start(out=w4_t[:, split:], in_=w4_words[0, :, split:])
+        nc.scalar.activation(out=warm[:], in_=warm[:], func=mybir.ActivationFunctionType.Identity)
+
+        def bias(j):
+            if j < 8:
+                return b_cols[0][:, 4 * j : 4 * j + 1]
+            return b_cols[1][:, 8 * (j - 8) : 8 * (j - 8) + 1]
+
+        def cast(engine_copy, h, c0, c1):
+            engine_copy(out=grouped[h][:, c0:c1, :], in_=raw[h][:, :, c0:c1].rearrange("p j t -> p t j"))
+
+        def quantize(h):
+            for c0 in range(0, HALF, QCOLS):
+                cols = slice(HALF * h + c0, HALF * h + c0 + QCOLS)
+                nc.vector.quantize_mx(
+                    out=codes[:, cols].bitcast(FP8X4),
+                    scales=scales[:, cols],
+                    in_=grouped[h][:, c0 : c0 + QCOLS, :].rearrange("p t j -> p (t j)"),
+                )
+
+        def prepare(h):
+            cast(nc.vector.tensor_copy, h, 0, QCOLS)
+            cast(nc.scalar.copy, h, V_COLS, HALF)
+            cast(nc.vector.tensor_copy, h, QCOLS, V_COLS)
+            quantize(h)
+
+        units = [(j, 0) for j in range(SOLO)]
+        units += [(j, h) for j in range(SOLO, TILES) for h in range(2)]
+        units += [(j, 1) for j in range(SOLO)]
+        accs = {}
+        results = {}
+
+        def matmul(u, rhs, rhs_scale, start, stop):
+            j = units[u][0]
+            nc.tensor.matmul_mx(
+                out=accs[u][:],
+                lhsT=w4_t[:, 2 * P * j : 2 * P * (j + 1)].bitcast(FP4X4),
+                lhsT_scale=w4_plane[:, P * j : P * (j + 1)],
+                rhs=rhs,
+                rhs_scale=rhs_scale,
+                start=start,
+                stop=stop,
+            )
+
+        def open_unit(u):
+            h = units[u][1]
+            acc = psum.tile([P, HALF], F32, name="acc")
+            accs[u] = acc
+            matmul(
+                u,
+                x4_t[:, T * h : T * (h + 1)].bitcast(FP4X4),
+                x4_plane[:, HALF * h : HALF * (h + 1)],
+                True,
+                False,
+            )
+
+        def close_unit(u):
+            h = units[u][1]
+            cols = slice(HALF * h, HALF * (h + 1))
+            matmul(u, codes[:, cols].bitcast(FP8X4), scales[:, cols], False, True)
+
+        def drain_unit(u):
+            j, h = units[u]
+            if j not in results:
+                o = outs.tile([P, T], F32, name="o", align_bytes=256)
+                results[j] = o
+            o = results[j]
+            cols = slice(HALF * h, HALF * (h + 1))
+            if u % 2 == 0:
+                nc.vector.tensor_scalar(
+                    out=o[:, cols],
+                    in0=accs[u][:],
+                    scalar1=bias(j),
+                    scalar2=None,
+                    op0=mybir.AluOpType.add,
+                )
+            else:
+                nc.scalar.activation(
+                    out=o[:, cols],
+                    in_=accs[u][:],
+                    func=mybir.ActivationFunctionType.Identity,
+                    bias=bias(j),
+                )
+            rows = slice(P * j, P * (j + 1))
+            if j < SOLO:
+                nc.sync.dma_start(out=out[rows, cols], in_=o[:, cols])
+            elif h == 1:
+                nc.sync.dma_start(out=out[rows, :], in_=o[:])
+
+        prepare(0)
+        nc.vector.transpose(b_cols[0][:], b_rows[0][:])
+        for u in range(LEAD):
+            open_unit(u)
+        for u in range(len(units)):
+            if u == SOLO:
+                prepare(1)
+                nc.vector.transpose(b_cols[1][:], b_rows[1][:])
+            close_unit(u)
+            drain_unit(u)
+            if u + LEAD < len(units):
+                open_unit(u + LEAD)

@@ -18,9 +18,9 @@ HALF = 512
 TILES = M // P
 FLOPS = 2 * 2 * K * M * T
 
-SOLO = 4
-LEAD = 4
-V_COLS = 320
+SOLO = 6
+LEAD = 3
+V_COLS = (320, 512)
 QCOLS = 256
 
 
@@ -60,12 +60,11 @@ def tile_mix_xres_fm_bias_kernel(tc, x4_words, x4_scales, xr, w4_words, w4_scale
         nc.vector.memset(b_rows[0][:], 0.0)
         nc.vector.memset(b_rows[1][:], 0.0)
 
-        def load_scales(queue, plane, rows):
-            for q in range(4):
-                queue.dma_start(
-                    out=plane[32 * q : 32 * q + 4, :].bitcast(I32),
-                    in_=rows[0, 4 * q : 4 * q + 4, :].bitcast(I32),
-                )
+        def load_scale_rows(queue, plane, rows, q):
+            queue.dma_start(
+                out=plane[32 * q : 32 * q + 4, :].bitcast(I32),
+                in_=rows[0, 4 * q : 4 * q + 4, :].bitcast(I32),
+            )
 
         def load_xr(h):
             nc.sync.dma_start(
@@ -75,15 +74,19 @@ def tile_mix_xres_fm_bias_kernel(tc, x4_words, x4_scales, xr, w4_words, w4_scale
 
         b_parts = b.rearrange("(k a i) -> a k i", a=4, i=32)
         split = 2 * P * SOLO
-        nc.sync.dma_start(out=w4_t[:, 0:split], in_=w4_words[0, :, 0:split])
-        nc.sync.dma_start(out=x4_t[:], in_=x4_words[0])
+        scale_rows = [(x4_plane, x4_scales, q) for q in range(4)] + [(w4_plane, w4_scales, q) for q in range(4)]
+        for plane, rows, q in scale_rows[:7]:
+            load_scale_rows(nc.scalar, plane, rows, q)
         load_xr(0)
-        load_scales(nc.scalar, x4_plane, x4_scales)
-        load_scales(nc.gpsimd, w4_plane, w4_scales)
-        nc.scalar.dma_start(out=b_rows[0][0:P:4, :], in_=b_parts[:, 0:8, :])
-        nc.gpsimd.dma_start(out=b_rows[1][0:P:8, :], in_=b_parts[:, 8:12, :])
-        load_xr(1)
+        for plane, rows, q in scale_rows[7:]:
+            load_scale_rows(nc.scalar, plane, rows, q)
+        nc.sync.dma_start(out=w4_t[:, 0:split], in_=w4_words[0, :, 0:split])
+        nc.sync.dma_start(out=x4_t[:, 0:T], in_=x4_words[0, :, 0:T])
         nc.sync.dma_start(out=w4_t[:, split:], in_=w4_words[0, :, split:])
+        nc.sync.dma_start(out=x4_t[:, T:], in_=x4_words[0, :, T:])
+        load_xr(1)
+        nc.scalar.dma_start(out=b_rows[0][0:P:4, :], in_=b_parts[:, 0:8, :])
+        nc.scalar.dma_start(out=b_rows[1][0:P:8, :], in_=b_parts[:, 8:12, :])
         nc.scalar.activation(out=warm[:], in_=warm[:], func=mybir.ActivationFunctionType.Identity)
 
         def bias(j):
@@ -105,8 +108,9 @@ def tile_mix_xres_fm_bias_kernel(tc, x4_words, x4_scales, xr, w4_words, w4_scale
 
         def prepare(h):
             cast(nc.vector.tensor_copy, h, 0, QCOLS)
-            cast(nc.scalar.copy, h, V_COLS, HALF)
-            cast(nc.vector.tensor_copy, h, QCOLS, V_COLS)
+            if V_COLS[h] < HALF:
+                cast(nc.scalar.copy, h, V_COLS[h], HALF)
+            cast(nc.vector.tensor_copy, h, QCOLS, V_COLS[h])
             quantize(h)
 
         units = [(j, 0) for j in range(SOLO)]
@@ -151,7 +155,7 @@ def tile_mix_xres_fm_bias_kernel(tc, x4_words, x4_scales, xr, w4_words, w4_scale
                 results[j] = o
             o = results[j]
             cols = slice(HALF * h, HALF * (h + 1))
-            if u % 2 == 0:
+            if u % 2 == 0 and u not in (4, 6):
                 nc.vector.tensor_scalar(
                     out=o[:, cols],
                     in0=accs[u][:],
@@ -177,7 +181,7 @@ def tile_mix_xres_fm_bias_kernel(tc, x4_words, x4_scales, xr, w4_words, w4_scale
         for u in range(LEAD):
             open_unit(u)
         for u in range(len(units)):
-            if u == SOLO:
+            if u == 4:
                 prepare(1)
                 nc.vector.transpose(b_cols[1][:], b_rows[1][:])
             close_unit(u)

@@ -9,19 +9,23 @@ I32 = mybir.dt.int32
 U8 = mybir.dt.uint8
 FP8X4 = mybir.dt.float8_e4m3fn_x4
 FP4X4 = mybir.dt.float4_e2m1fn_x4
+ADD = mybir.AluOpType.add
+IDENTITY = mybir.ActivationFunctionType.Identity
 
 P = 128
-K = 512
+PACK = 4
+K = P * PACK
 M = 1536
 T = 1024
-HALF = 512
+HALF = T // 2
 TILES = M // P
+BANKS = 8
 FLOPS = 2 * 2 * K * M * T
 
-SOLO = 6
-LEAD = 3
-V_COLS = (320, 512)
-QCOLS = 256
+SOLO = 7
+HEAD = 3
+LEAD = 5
+FIRST = 384
 
 
 def tile_mix_xres_fm_bias_kernel(tc, x4_words, x4_scales, xr, w4_words, w4_scales, b, out):
@@ -29,36 +33,30 @@ def tile_mix_xres_fm_bias_kernel(tc, x4_words, x4_scales, xr, w4_words, w4_scale
     with ExitStack() as ctx:
         keep = ctx.enter_context(tc.tile_pool(name="keep", bufs=1))
         outs = ctx.enter_context(tc.tile_pool(name="outs", bufs=TILES))
-        psum = ctx.enter_context(tc.psum_pool(name="psum", bufs=8))
+        psum = ctx.enter_context(tc.psum_pool(name="psum", bufs=BANKS))
         ctx.enter_context(tc.manual_schedule())
 
         warm = keep.tile([P, 1], F32, name="warm")
-        x4_plane = keep.tile([P, T], U8, name="x4_plane", align_bytes=256)
+        w4 = keep.tile([P, 2 * M], U8, name="w4", align_bytes=256)
         w4_plane = keep.tile([P, M], U8, name="w4_plane", align_bytes=256)
-        b_rows = []
-        b_cols = []
-        for i in range(2):
-            rows = keep.tile([P, 32], F32, name="b_rows%d" % i, align_bytes=256)
-            cols = keep.tile([P, 32], F32, name="b_cols%d" % i, align_bytes=256)
-            b_rows.append(rows)
-            b_cols.append(cols)
-        x4_t = keep.tile([P, 2 * T], U8, name="x4_t", align_bytes=256)
-        w4_t = keep.tile([P, 2 * M], U8, name="w4_t", align_bytes=256)
+        x4 = keep.tile([P, 2 * T], U8, name="x4", align_bytes=256)
+        x4_plane = keep.tile([P, T], U8, name="x4_plane", align_bytes=256)
         codes = keep.tile([P, T], U32, name="codes", align_bytes=256)
         scales = keep.tile([P, T], U8, name="scales", align_bytes=256)
-        raw = []
-        grouped = []
-        for h in range(2):
-            r = keep.tile([P, 4, HALF], F32, name="raw%d" % h, align_bytes=256)
-            g = keep.tile([P, HALF, 4], BF16, name="grouped%d" % h, align_bytes=256)
-            raw.append(r)
-            grouped.append(g)
+        raw_a = keep.tile([P, PACK, FIRST], F32, name="raw_a", align_bytes=256)
+        raw_b = keep.tile([P, PACK, HALF - FIRST], F32, name="raw_b", align_bytes=256)
+        raw_c = keep.tile([P, PACK, HALF], F32, name="raw_c", align_bytes=256)
+        grouped = keep.tile([P, T, PACK], BF16, name="grouped", align_bytes=256)
+        b_rows_lo = keep.tile([P, 32], F32, name="b_rows_lo", align_bytes=256)
+        b_rows_hi = keep.tile([P, 32], F32, name="b_rows_hi", align_bytes=256)
+        b_cols_lo = keep.tile([P, 32], F32, name="b_cols_lo", align_bytes=256)
+        b_cols_hi = keep.tile([P, 32], F32, name="b_cols_hi", align_bytes=256)
 
+        nc.gpsimd.memset(w4_plane[:].bitcast(I32), 0)
+        nc.gpsimd.memset(x4_plane[:].bitcast(I32), 0)
         nc.vector.memset(warm[:], 0.0)
-        nc.vector.memset(x4_plane[:].bitcast(I32), 0)
-        nc.vector.memset(w4_plane[:].bitcast(I32), 0)
-        nc.vector.memset(b_rows[0][:], 0.0)
-        nc.vector.memset(b_rows[1][:], 0.0)
+        nc.vector.memset(b_rows_lo[:], 0.0)
+        nc.vector.memset(b_rows_hi[:], 0.0)
 
         def load_scale_rows(queue, plane, rows, q):
             queue.dma_start(
@@ -66,52 +64,55 @@ def tile_mix_xres_fm_bias_kernel(tc, x4_words, x4_scales, xr, w4_words, w4_scale
                 in_=rows[0, 4 * q : 4 * q + 4, :].bitcast(I32),
             )
 
-        def load_xr(h):
-            nc.sync.dma_start(
-                out=raw[h][:],
-                in_=xr[:, HALF * h : HALF * (h + 1)].rearrange("(p j) t -> p j t", j=4),
-            )
+        def load_xr(tile, t0, t1):
+            nc.sync.dma_start(out=tile[:], in_=xr[:, t0:t1].rearrange("(p j) t -> p j t", j=PACK))
 
-        b_parts = b.rearrange("(k a i) -> a k i", a=4, i=32)
-        split = 2 * P * SOLO
-        scale_rows = [(x4_plane, x4_scales, q) for q in range(4)] + [(w4_plane, w4_scales, q) for q in range(4)]
-        for plane, rows, q in scale_rows[:7]:
-            load_scale_rows(nc.scalar, plane, rows, q)
-        load_xr(0)
-        for plane, rows, q in scale_rows[7:]:
-            load_scale_rows(nc.scalar, plane, rows, q)
-        nc.sync.dma_start(out=w4_t[:, 0:split], in_=w4_words[0, :, 0:split])
-        nc.sync.dma_start(out=x4_t[:, 0:T], in_=x4_words[0, :, 0:T])
-        nc.sync.dma_start(out=w4_t[:, split:], in_=w4_words[0, :, split:])
-        nc.sync.dma_start(out=x4_t[:, T:], in_=x4_words[0, :, T:])
-        load_xr(1)
-        nc.scalar.dma_start(out=b_rows[0][0:P:4, :], in_=b_parts[:, 0:8, :])
-        nc.scalar.dma_start(out=b_rows[1][0:P:8, :], in_=b_parts[:, 8:12, :])
-        nc.scalar.activation(out=warm[:], in_=warm[:], func=mybir.ActivationFunctionType.Identity)
+        nc.sync.dma_start(out=w4[:], in_=w4_words[0])
+        nc.gpsimd.dma_start(out=x4[:, 0:T].bitcast(I32), in_=x4_words[0, :, 0:T].bitcast(I32))
+        for q in range(4):
+            load_scale_rows(nc.sync, w4_plane, w4_scales, q)
+        load_scale_rows(nc.scalar, x4_plane, x4_scales, 0)
+        load_xr(raw_a, 0, FIRST)
+        load_xr(raw_b, FIRST, HALF)
+        nc.scalar.activation(out=warm[:], in_=warm[:], func=IDENTITY)
+        for q in range(1, 4):
+            load_scale_rows(nc.scalar, x4_plane, x4_scales, q)
+        b_rows = b.rearrange("(k a i) -> a k i", a=4, i=32)
+        nc.gpsimd.dma_start(out=b_rows_lo[0:P:4, :], in_=b_rows[:, 0:8, :])
+        nc.gpsimd.dma_start(out=b_rows_hi[0:P:8, :], in_=b_rows[:, 8:12, :])
+        nc.sync.dma_start(out=x4[:, T:], in_=x4_words[0, :, T:])
+        load_xr(raw_c, HALF, T)
 
         def bias(j):
             if j < 8:
-                return b_cols[0][:, 4 * j : 4 * j + 1]
-            return b_cols[1][:, 8 * (j - 8) : 8 * (j - 8) + 1]
+                return b_cols_lo[:, 4 * j : 4 * j + 1]
+            return b_cols_hi[:, 8 * (j - 8) : 8 * (j - 8) + 1]
 
-        def cast(engine_copy, h, c0, c1):
-            engine_copy(out=grouped[h][:, c0:c1, :], in_=raw[h][:, :, c0:c1].rearrange("p j t -> p t j"))
+        def cast(copy, tile, origin, t0, t1):
+            copy(out=grouped[:, t0:t1, :], in_=tile[:, :, t0 - origin : t1 - origin].rearrange("p j t -> p t j"))
 
-        def quantize(h):
-            for c0 in range(0, HALF, QCOLS):
-                cols = slice(HALF * h + c0, HALF * h + c0 + QCOLS)
-                nc.vector.quantize_mx(
-                    out=codes[:, cols].bitcast(FP8X4),
-                    scales=scales[:, cols],
-                    in_=grouped[h][:, c0 : c0 + QCOLS, :].rearrange("p t j -> p (t j)"),
-                )
+        def quantize(t0, t1):
+            nc.vector.quantize_mx(
+                out=codes[:, t0:t1].bitcast(FP8X4),
+                scales=scales[:, t0:t1],
+                in_=grouped[:, t0:t1, :].rearrange("p t j -> p (t j)"),
+            )
 
-        def prepare(h):
-            cast(nc.vector.tensor_copy, h, 0, QCOLS)
-            if V_COLS[h] < HALF:
-                cast(nc.scalar.copy, h, V_COLS[h], HALF)
-            cast(nc.vector.tensor_copy, h, QCOLS, V_COLS[h])
-            quantize(h)
+        def prepare_first_half():
+            cast(nc.vector.tensor_copy, raw_a, 0, 0, 256)
+            cast(nc.scalar.copy, raw_a, 0, 256, FIRST)
+            quantize(0, 256)
+            quantize(256, FIRST)
+            cast(nc.vector.tensor_copy, raw_b, FIRST, FIRST, HALF)
+            quantize(FIRST, HALF)
+            nc.vector.transpose(b_cols_lo[:], b_rows_lo[:])
+
+        def prepare_second_half():
+            cast(nc.vector.tensor_copy, raw_c, HALF, 512, 768)
+            cast(nc.vector.tensor_copy, raw_c, HALF, 768, 1024)
+            quantize(512, 768)
+            quantize(768, 1024)
+            nc.vector.transpose(b_cols_hi[:], b_rows_hi[:])
 
         units = [(j, 0) for j in range(SOLO)]
         units += [(j, h) for j in range(SOLO, TILES) for h in range(2)]
@@ -119,11 +120,11 @@ def tile_mix_xres_fm_bias_kernel(tc, x4_words, x4_scales, xr, w4_words, w4_scale
         accs = {}
         results = {}
 
-        def matmul(u, rhs, rhs_scale, start, stop):
+        def add_product(u, rhs, rhs_scale, start, stop):
             j = units[u][0]
             nc.tensor.matmul_mx(
                 out=accs[u][:],
-                lhsT=w4_t[:, 2 * P * j : 2 * P * (j + 1)].bitcast(FP4X4),
+                lhsT=w4[:, 2 * P * j : 2 * P * (j + 1)].bitcast(FP4X4),
                 lhsT_scale=w4_plane[:, P * j : P * (j + 1)],
                 rhs=rhs,
                 rhs_scale=rhs_scale,
@@ -135,18 +136,14 @@ def tile_mix_xres_fm_bias_kernel(tc, x4_words, x4_scales, xr, w4_words, w4_scale
             h = units[u][1]
             acc = psum.tile([P, HALF], F32, name="acc")
             accs[u] = acc
-            matmul(
-                u,
-                x4_t[:, T * h : T * (h + 1)].bitcast(FP4X4),
-                x4_plane[:, HALF * h : HALF * (h + 1)],
-                True,
-                False,
-            )
+            words = slice(2 * HALF * h, 2 * HALF * (h + 1))
+            cols = slice(HALF * h, HALF * (h + 1))
+            add_product(u, x4[:, words].bitcast(FP4X4), x4_plane[:, cols], True, False)
 
         def close_unit(u):
             h = units[u][1]
             cols = slice(HALF * h, HALF * (h + 1))
-            matmul(u, codes[:, cols].bitcast(FP8X4), scales[:, cols], False, True)
+            add_product(u, codes[:, cols].bitcast(FP8X4), scales[:, cols], False, True)
 
         def drain_unit(u):
             j, h = units[u]
@@ -155,36 +152,25 @@ def tile_mix_xres_fm_bias_kernel(tc, x4_words, x4_scales, xr, w4_words, w4_scale
                 results[j] = o
             o = results[j]
             cols = slice(HALF * h, HALF * (h + 1))
-            if u % 2 == 0 and u not in (4, 6):
-                nc.vector.tensor_scalar(
-                    out=o[:, cols],
-                    in0=accs[u][:],
-                    scalar1=bias(j),
-                    scalar2=None,
-                    op0=mybir.AluOpType.add,
-                )
+            if u in (0, 2, 7) or (u >= 8 and u % 2 == 0):
+                nc.vector.tensor_scalar(out=o[:, cols], in0=accs[u][:], scalar1=bias(j), scalar2=None, op0=ADD)
             else:
-                nc.scalar.activation(
-                    out=o[:, cols],
-                    in_=accs[u][:],
-                    func=mybir.ActivationFunctionType.Identity,
-                    bias=bias(j),
-                )
+                nc.scalar.activation(out=o[:, cols], in_=accs[u][:], func=IDENTITY, bias=bias(j))
             rows = slice(P * j, P * (j + 1))
             if j < SOLO:
                 nc.sync.dma_start(out=out[rows, cols], in_=o[:, cols])
             elif h == 1:
                 nc.sync.dma_start(out=out[rows, :], in_=o[:])
 
-        prepare(0)
-        nc.vector.transpose(b_cols[0][:], b_rows[0][:])
-        for u in range(LEAD):
+        prepare_first_half()
+        for u in range(HEAD):
             open_unit(u)
+        opened = HEAD
         for u in range(len(units)):
             if u == 4:
-                prepare(1)
-                nc.vector.transpose(b_cols[1][:], b_rows[1][:])
+                prepare_second_half()
             close_unit(u)
             drain_unit(u)
-            if u + LEAD < len(units):
-                open_unit(u + LEAD)
+            while opened < min(len(units), u + 1 + min(LEAD, HEAD + u // 2)):
+                open_unit(opened)
+                opened += 1

@@ -23,9 +23,7 @@ BANKS = 8
 FLOPS = 2 * 2 * K * M * T
 
 SOLO = 7
-HEAD = 3
 LEAD = 5
-FIRST = 384
 
 
 def tile_mix_xres_fm_bias_kernel(tc, x4_words, x4_scales, xr, w4_words, w4_scales, b, out):
@@ -36,27 +34,24 @@ def tile_mix_xres_fm_bias_kernel(tc, x4_words, x4_scales, xr, w4_words, w4_scale
         psum = ctx.enter_context(tc.psum_pool(name="psum", bufs=BANKS))
         ctx.enter_context(tc.manual_schedule())
 
-        warm = keep.tile([P, 1], F32, name="warm")
+        zeros = keep.tile([P, 32], F32, name="zeros", align_bytes=256)
         w4 = keep.tile([P, 2 * M], U8, name="w4", align_bytes=256)
         w4_plane = keep.tile([P, M], U8, name="w4_plane", align_bytes=256)
         x4 = keep.tile([P, 2 * T], U8, name="x4", align_bytes=256)
         x4_plane = keep.tile([P, T], U8, name="x4_plane", align_bytes=256)
         codes = keep.tile([P, T], U32, name="codes", align_bytes=256)
         scales = keep.tile([P, T], U8, name="scales", align_bytes=256)
-        raw_a = keep.tile([P, PACK, FIRST], F32, name="raw_a", align_bytes=256)
-        raw_b = keep.tile([P, PACK, HALF - FIRST], F32, name="raw_b", align_bytes=256)
-        raw_c = keep.tile([P, PACK, HALF], F32, name="raw_c", align_bytes=256)
+        raw_lo = keep.tile([P, PACK, HALF], F32, name="raw_lo", align_bytes=256)
+        raw_hi = keep.tile([P, PACK, HALF], F32, name="raw_hi", align_bytes=256)
         grouped = keep.tile([P, T, PACK], BF16, name="grouped", align_bytes=256)
         b_rows_lo = keep.tile([P, 32], F32, name="b_rows_lo", align_bytes=256)
         b_rows_hi = keep.tile([P, 32], F32, name="b_rows_hi", align_bytes=256)
         b_cols_lo = keep.tile([P, 32], F32, name="b_cols_lo", align_bytes=256)
         b_cols_hi = keep.tile([P, 32], F32, name="b_cols_hi", align_bytes=256)
 
-        nc.gpsimd.memset(w4_plane[:].bitcast(I32), 0)
+        nc.vector.memset(w4_plane[:].bitcast(I32), 0)
         nc.gpsimd.memset(x4_plane[:].bitcast(I32), 0)
-        nc.vector.memset(warm[:], 0.0)
-        nc.vector.memset(b_rows_lo[:], 0.0)
-        nc.vector.memset(b_rows_hi[:], 0.0)
+        nc.vector.memset(zeros[:], 0.0)
 
         def load_scale_rows(queue, plane, rows, q):
             queue.dma_start(
@@ -64,24 +59,23 @@ def tile_mix_xres_fm_bias_kernel(tc, x4_words, x4_scales, xr, w4_words, w4_scale
                 in_=rows[0, 4 * q : 4 * q + 4, :].bitcast(I32),
             )
 
-        def load_xr(tile, t0, t1):
-            nc.sync.dma_start(out=tile[:], in_=xr[:, t0:t1].rearrange("(p j) t -> p j t", j=PACK))
+        def load_xr(queue, tile, t0, t1):
+            queue.dma_start(out=tile[:], in_=xr[:, t0:t1].rearrange("(p j) t -> p j t", j=PACK))
 
+        load_xr(nc.sync, raw_lo, 0, HALF)
         nc.sync.dma_start(out=w4[:], in_=w4_words[0])
-        nc.gpsimd.dma_start(out=x4[:, 0:T].bitcast(I32), in_=x4_words[0, :, 0:T].bitcast(I32))
+        nc.sync.dma_start(out=x4[:], in_=x4_words[0])
         for q in range(4):
-            load_scale_rows(nc.sync, w4_plane, w4_scales, q)
+            load_scale_rows(nc.scalar, w4_plane, w4_scales, q)
         load_scale_rows(nc.scalar, x4_plane, x4_scales, 0)
-        load_xr(raw_a, 0, FIRST)
-        load_xr(raw_b, FIRST, HALF)
-        nc.scalar.activation(out=warm[:], in_=warm[:], func=IDENTITY)
         for q in range(1, 4):
-            load_scale_rows(nc.scalar, x4_plane, x4_scales, q)
+            load_scale_rows(nc.gpsimd, x4_plane, x4_scales, q)
+        load_xr(nc.gpsimd, raw_hi, HALF, T)
+        nc.scalar.activation(out=b_rows_lo[:], in_=zeros[:], func=IDENTITY)
+        nc.scalar.activation(out=b_rows_hi[:], in_=zeros[:], func=IDENTITY)
         b_rows = b.rearrange("(k a i) -> a k i", a=4, i=32)
-        nc.gpsimd.dma_start(out=b_rows_lo[0:P:4, :], in_=b_rows[:, 0:8, :])
-        nc.gpsimd.dma_start(out=b_rows_hi[0:P:8, :], in_=b_rows[:, 8:12, :])
-        nc.sync.dma_start(out=x4[:, T:], in_=x4_words[0, :, T:])
-        load_xr(raw_c, HALF, T)
+        nc.sync.dma_start(out=b_rows_lo[0:P:4, :], in_=b_rows[:, 0:8, :])
+        nc.sync.dma_start(out=b_rows_hi[0:P:8, :], in_=b_rows[:, 8:12, :])
 
         def bias(j):
             if j < 8:
@@ -99,17 +93,16 @@ def tile_mix_xres_fm_bias_kernel(tc, x4_words, x4_scales, xr, w4_words, w4_scale
             )
 
         def prepare_first_half():
-            cast(nc.vector.tensor_copy, raw_a, 0, 0, 256)
-            cast(nc.scalar.copy, raw_a, 0, 256, FIRST)
+            cast(nc.vector.tensor_copy, raw_lo, 0, 0, 256)
+            cast(nc.scalar.copy, raw_lo, 0, 320, 512)
+            cast(nc.vector.tensor_copy, raw_lo, 0, 256, 320)
             quantize(0, 256)
-            quantize(256, FIRST)
-            cast(nc.vector.tensor_copy, raw_b, FIRST, FIRST, HALF)
-            quantize(FIRST, HALF)
+            quantize(256, 512)
             nc.vector.transpose(b_cols_lo[:], b_rows_lo[:])
 
         def prepare_second_half():
-            cast(nc.vector.tensor_copy, raw_c, HALF, 512, 768)
-            cast(nc.vector.tensor_copy, raw_c, HALF, 768, 1024)
+            cast(nc.vector.tensor_copy, raw_hi, HALF, 512, 768)
+            cast(nc.vector.tensor_copy, raw_hi, HALF, 768, 1024)
             quantize(512, 768)
             quantize(768, 1024)
             nc.vector.transpose(b_cols_hi[:], b_rows_hi[:])
@@ -132,18 +125,30 @@ def tile_mix_xres_fm_bias_kernel(tc, x4_words, x4_scales, xr, w4_words, w4_scale
                 stop=stop,
             )
 
-        def open_unit(u):
+        def add_x4(u, start):
             h = units[u][1]
-            acc = psum.tile([P, HALF], F32, name="acc")
-            accs[u] = acc
             words = slice(2 * HALF * h, 2 * HALF * (h + 1))
             cols = slice(HALF * h, HALF * (h + 1))
-            add_product(u, x4[:, words].bitcast(FP4X4), x4_plane[:, cols], True, False)
+            add_product(u, x4[:, words].bitcast(FP4X4), x4_plane[:, cols], start, not start)
 
-        def close_unit(u):
+        def add_xr(u, start):
             h = units[u][1]
             cols = slice(HALF * h, HALF * (h + 1))
-            add_product(u, codes[:, cols].bitcast(FP8X4), scales[:, cols], False, True)
+            add_product(u, codes[:, cols].bitcast(FP8X4), scales[:, cols], start, not start)
+
+        def open_unit(u):
+            acc = psum.tile([P, HALF], F32, name="acc")
+            accs[u] = acc
+            if units[u][1] == 0:
+                add_xr(u, True)
+            else:
+                add_x4(u, True)
+
+        def close_unit(u):
+            if units[u][1] == 0:
+                add_x4(u, False)
+            else:
+                add_xr(u, False)
 
         def drain_unit(u):
             j, h = units[u]
@@ -163,14 +168,12 @@ def tile_mix_xres_fm_bias_kernel(tc, x4_words, x4_scales, xr, w4_words, w4_scale
                 nc.sync.dma_start(out=out[rows, :], in_=o[:])
 
         prepare_first_half()
-        for u in range(HEAD):
-            open_unit(u)
-        opened = HEAD
+        opened = 0
         for u in range(len(units)):
+            while opened < min(len(units), u + 1 + min(LEAD, u // 2)):
+                open_unit(opened)
+                opened += 1
             if u == 4:
                 prepare_second_half()
             close_unit(u)
             drain_unit(u)
-            while opened < min(len(units), u + 1 + min(LEAD, HEAD + u // 2)):
-                open_unit(opened)
-                opened += 1

from contextlib import ExitStack

import concourse.mybir as mybir

F32 = mybir.dt.float32
BF16 = mybir.dt.bfloat16
U32 = mybir.dt.uint32
I32 = mybir.dt.int32
U8 = mybir.dt.uint8
FP8X4 = mybir.dt.float8_e4m3fn_x4
FP4X4 = mybir.dt.float4_e2m1fn_x4
ADD = mybir.AluOpType.add
IDENTITY = mybir.ActivationFunctionType.Identity

P = 128
PACK = 4
K = P * PACK
M = 1536
T = 1024
HALF = T // 2
TILES = M // P
BANKS = 8
FLOPS = 2 * 2 * K * M * T

SOLO = 7
LEAD = 5


def tile_mix_xres_fm_bias_kernel(tc, x4_words, x4_scales, xr, w4_words, w4_scales, b, out):
    nc = tc.nc
    with ExitStack() as ctx:
        keep = ctx.enter_context(tc.tile_pool(name="keep", bufs=1))
        outs = ctx.enter_context(tc.tile_pool(name="outs", bufs=TILES))
        psum = ctx.enter_context(tc.psum_pool(name="psum", bufs=BANKS))
        ctx.enter_context(tc.manual_schedule())

        zeros = keep.tile([P, 32], F32, name="zeros", align_bytes=256)
        w4 = keep.tile([P, 2 * M], U8, name="w4", align_bytes=256)
        w4_plane = keep.tile([P, M], U8, name="w4_plane", align_bytes=256)
        x4 = keep.tile([P, 2 * T], U8, name="x4", align_bytes=256)
        x4_plane = keep.tile([P, T], U8, name="x4_plane", align_bytes=256)
        codes = keep.tile([P, T], U32, name="codes", align_bytes=256)
        scales = keep.tile([P, T], U8, name="scales", align_bytes=256)
        raw_lo = keep.tile([P, PACK, HALF], F32, name="raw_lo", align_bytes=256)
        raw_hi = keep.tile([P, PACK, HALF], F32, name="raw_hi", align_bytes=256)
        grouped = keep.tile([P, T, PACK], BF16, name="grouped", align_bytes=256)
        b_rows_lo = keep.tile([P, 32], F32, name="b_rows_lo", align_bytes=256)
        b_rows_hi = keep.tile([P, 32], F32, name="b_rows_hi", align_bytes=256)
        b_cols_lo = keep.tile([P, 32], F32, name="b_cols_lo", align_bytes=256)
        b_cols_hi = keep.tile([P, 32], F32, name="b_cols_hi", align_bytes=256)

        nc.vector.memset(w4_plane[:].bitcast(I32), 0)
        nc.gpsimd.memset(x4_plane[:].bitcast(I32), 0)
        nc.vector.memset(zeros[:], 0.0)

        def load_scale_rows(queue, plane, rows, q):
            queue.dma_start(
                out=plane[32 * q : 32 * q + 4, :].bitcast(I32),
                in_=rows[0, 4 * q : 4 * q + 4, :].bitcast(I32),
            )

        def load_xr(queue, tile, t0, t1):
            queue.dma_start(out=tile[:], in_=xr[:, t0:t1].rearrange("(p j) t -> p j t", j=PACK))

        load_xr(nc.sync, raw_lo, 0, HALF)
        nc.sync.dma_start(out=w4[:], in_=w4_words[0])
        nc.sync.dma_start(out=x4[:], in_=x4_words[0])
        for q in range(4):
            load_scale_rows(nc.scalar, w4_plane, w4_scales, q)
        load_scale_rows(nc.scalar, x4_plane, x4_scales, 0)
        for q in range(1, 4):
            load_scale_rows(nc.gpsimd, x4_plane, x4_scales, q)
        load_xr(nc.gpsimd, raw_hi, HALF, T)
        nc.scalar.activation(out=b_rows_lo[:], in_=zeros[:], func=IDENTITY)
        nc.scalar.activation(out=b_rows_hi[:], in_=zeros[:], func=IDENTITY)
        b_rows = b.rearrange("(k a i) -> a k i", a=4, i=32)
        nc.sync.dma_start(out=b_rows_lo[0:P:4, :], in_=b_rows[:, 0:8, :])
        nc.sync.dma_start(out=b_rows_hi[0:P:8, :], in_=b_rows[:, 8:12, :])

        def bias(j):
            if j < 8:
                return b_cols_lo[:, 4 * j : 4 * j + 1]
            return b_cols_hi[:, 8 * (j - 8) : 8 * (j - 8) + 1]

        def cast(copy, tile, origin, t0, t1):
            copy(out=grouped[:, t0:t1, :], in_=tile[:, :, t0 - origin : t1 - origin].rearrange("p j t -> p t j"))

        def quantize(t0, t1):
            nc.vector.quantize_mx(
                out=codes[:, t0:t1].bitcast(FP8X4),
                scales=scales[:, t0:t1],
                in_=grouped[:, t0:t1, :].rearrange("p t j -> p (t j)"),
            )

        def prepare_first_half():
            cast(nc.vector.tensor_copy, raw_lo, 0, 0, 256)
            cast(nc.scalar.copy, raw_lo, 0, 320, 512)
            cast(nc.vector.tensor_copy, raw_lo, 0, 256, 320)
            quantize(0, 256)
            quantize(256, 512)
            nc.vector.transpose(b_cols_lo[:], b_rows_lo[:])

        def prepare_second_half():
            cast(nc.vector.tensor_copy, raw_hi, HALF, 512, 768)
            cast(nc.vector.tensor_copy, raw_hi, HALF, 768, 1024)
            quantize(512, 768)
            quantize(768, 1024)
            nc.vector.transpose(b_cols_hi[:], b_rows_hi[:])

        units = [(j, 0) for j in range(SOLO)]
        units += [(j, h) for j in range(SOLO, TILES) for h in range(2)]
        units += [(j, 1) for j in range(SOLO)]
        accs = {}
        results = {}

        def add_product(u, rhs, rhs_scale, start, stop):
            j = units[u][0]
            nc.tensor.matmul_mx(
                out=accs[u][:],
                lhsT=w4[:, 2 * P * j : 2 * P * (j + 1)].bitcast(FP4X4),
                lhsT_scale=w4_plane[:, P * j : P * (j + 1)],
                rhs=rhs,
                rhs_scale=rhs_scale,
                start=start,
                stop=stop,
            )

        def add_x4(u, start):
            h = units[u][1]
            words = slice(2 * HALF * h, 2 * HALF * (h + 1))
            cols = slice(HALF * h, HALF * (h + 1))
            add_product(u, x4[:, words].bitcast(FP4X4), x4_plane[:, cols], start, not start)

        def add_xr(u, start):
            h = units[u][1]
            cols = slice(HALF * h, HALF * (h + 1))
            add_product(u, codes[:, cols].bitcast(FP8X4), scales[:, cols], start, not start)

        def open_unit(u):
            acc = psum.tile([P, HALF], F32, name="acc")
            accs[u] = acc
            if units[u][1] == 0:
                add_xr(u, True)
            else:
                add_x4(u, True)

        def close_unit(u):
            if units[u][1] == 0:
                add_x4(u, False)
            else:
                add_xr(u, False)

        def drain_unit(u):
            j, h = units[u]
            if j not in results:
                o = outs.tile([P, T], F32, name="o", align_bytes=256)
                results[j] = o
            o = results[j]
            cols = slice(HALF * h, HALF * (h + 1))
            if u in (0, 2, 7) or (u >= 8 and u % 2 == 0):
                nc.vector.tensor_scalar(out=o[:, cols], in0=accs[u][:], scalar1=bias(j), scalar2=None, op0=ADD)
            else:
                nc.scalar.activation(out=o[:, cols], in_=accs[u][:], func=IDENTITY, bias=bias(j))
            rows = slice(P * j, P * (j + 1))
            if j < SOLO:
                nc.sync.dma_start(out=out[rows, cols], in_=o[:, cols])
            elif h == 1:
                nc.sync.dma_start(out=out[rows, :], in_=o[:])

        prepare_first_half()
        opened = 0
        for u in range(len(units)):
            while opened < min(len(units), u + 1 + min(LEAD, u // 2)):
                open_unit(opened)
                opened += 1
            if u == 4:
                prepare_second_half()
            close_unit(u)
            drain_unit(u)
